import numpy as np
import ml_dtypes


def mxq(x, axis, fmt="e4m3"):
    dtype, down = {"e4m3": (ml_dtypes.float8_e4m3fn, 7), "e5m2": (ml_dtypes.float8_e5m2, 14)}[fmt]
    v = np.moveaxis(np.asarray(x, np.float32).astype(ml_dtypes.bfloat16).astype(np.float64), axis, -1)
    blocks = v.reshape(v.shape[:-1] + (-1, 32))
    amax = np.abs(blocks).max(-1, keepdims=True)
    byte = np.maximum(np.where(amax > 0, np.frexp(amax)[1] - 1 + 127, 0) - down, 1)
    scale = np.exp2(byte - 127.0)
    codes = (blocks / scale).astype(np.float32).astype(dtype).astype(np.float64)
    return np.moveaxis((codes * scale).reshape(v.shape), -1, axis)


WIDE = False


def mx_kscale(k):
    if not WIDE:
        return np.ones(k)
    levels = np.array([10, -10, 5, -5, 0])
    if k % 512:
        return np.exp2(np.random.permutation(np.resize(levels, k // 32))).repeat(32)
    a = np.empty((k // 512, 16))
    for p in range(k // 512):
        a[p, :8] = np.random.permutation(np.resize(levels, 8))
        for g in range(8):
            far = levels[np.abs(levels - a[p, g]) >= 10]
            a[p, g + 8] = far[np.random.randint(len(far))]
    return np.exp2(a.ravel()).repeat(32)


BF16 = ml_dtypes.bfloat16


def bf(x):
    return np.asarray(x, np.float32).astype(BF16)


def f64(x):
    return np.asarray(x).astype(np.float64)

def planes(Y):
    n, m = Y.shape
    b = f64(bf(Y)).reshape(n // 32, 32, m)
    amax = np.abs(b).max(1)
    byte = np.clip(np.where(amax > 0, np.frexp(amax)[1] - 1 + 127 - 7, 1), 1, 254)
    codes = (b * np.exp2(127.0 - byte)[:, None, :]).reshape(n, m).astype(np.float32).astype(ml_dtypes.float8_e4m3fn).view(np.uint8)
    words = codes.reshape(n // 512, 128, 4, m).transpose(0, 1, 3, 2)
    return np.ascontiguousarray(words), np.ascontiguousarray(byte.astype(np.uint8).reshape(n // 512, 16, m))


B, T, D, F, S = 4, 1024, 512, 1024, 512


def setup_inputs():
    s = mx_kscale(D)
    t = mx_kscale(T)
    obs = np.random.randn(B, T, D) * s
    w_in = np.random.randn(D, F) / np.sqrt(D) / s[:, None]
    step_gain = np.exp(0.3 * np.random.randn(T)) * t
    w_time = 1.5 * np.random.randn(T, S) / np.sqrt(T) / t[:, None]
    bias = 0.4 * np.random.randn(F)
    gain = np.exp(0.8 * np.random.randn(F))
    return {"obs": bf(obs), "w_in": bf(w_in), "step_gain": bf(step_gain),
            "w_time": bf(w_time), "bias": bf(bias), "gain": bf(gain)}


def reference(obs, w_in, step_gain, w_time, bias, gain):
    x = mxq(f64(obs), 2, "e4m3")
    w1 = mxq(f64(w_in), 0, "e4m3")
    a = x @ w1
    h = np.tanh(a) * f64(step_gain)[:, None]
    w2 = mxq(f64(w_time), 0, "e4m3")
    hq = mxq(h, 1, "e4m3")
    z = w2.T @ hq
    y = np.tanh(z + f64(bias)) * f64(gain)
    Y = y.reshape(B * S, F).T
    words, scales = planes(Y)
    return y, words, scales

from contextlib import ExitStack

import concourse.mybir as mybir
from concourse.masks import make_identity

B, T, D, F, S = 4, 1024, 512, 1024, 512
FLOPS = 2 * B * T * D * F + 2 * B * S * T * F

F32 = mybir.dt.float32
BF16 = mybir.dt.bfloat16
I32 = mybir.dt.int32
U32 = mybir.dt.uint32
U8 = mybir.dt.uint8
FP8X4 = mybir.dt.float8_e4m3fn_x4
TANH = mybir.ActivationFunctionType.Tanh
MULT = mybir.AluOpType.mult

P = 128
PACK = 4
K_PASS = P * PACK
BANK = 512
BANKS = 7
CHUNK = 256
STEPS = B * F // CHUNK


POOL_COLS = 176
DVE_TURNS = (1,)
X_LEAD = 6


def program_order():
    order = [
        ("load_x", 0, 0),
        ("load_w_in", 0),
        ("load_x", 0, 1),
        ("load_vectors",),
        ("load_x", 1, None),
        ("load_w_in", 1),
        ("load_w_time", 0),
        ("load_w_time", 1),
    ]
    add = order.append
    for half in range(2, 2 * B):
        add(("load_x", half, None))
    order.extend(
        [
            ("turn_x", 0),
            ("empty_x", 0, "act"),
            ("group_w_in", 0, "dve"),
            ("group_w_in", 1, "act"),
            ("quant_x", 0, 0),
            ("quant_w_in", 0),
            ("turn_x", 1),
            ("layer1", 0, 0, 0),
            ("empty_x", 1, "dve"),
            ("quant_w_in", 1),
            ("quant_x", 0, 1),
            ("layer1", 1, 0, 0),
            ("vectors",),
            ("layer1", 0, 0, 1),
            ("layer1", 1, 0, 1),
            ("turn_x", 2),
            ("turn_x", 3),
            ("empty_x", 2, "act"),
            ("empty_x", 3, "act"),
            ("group_w_in", 2, "dve"),
            ("step_gain", 0, 0, 0),
            ("group_w_in", 3, "dve"),
            ("quant_x", 1, None),
            ("quant_h", 0, 0),
            ("group_w_time", 0, "act"),
            ("layer1", 0, 1, 0),
            ("layer1", 0, 1, 1),
            ("layer1", 1, 1, 0),
            ("layer1", 1, 1, 1),
            ("quant_w_in", 2),
            ("quant_w_in", 3),
            ("step_gain", 1, 0, 0),
            ("step_gain", 0, 1, 0),
            ("group_w_time", 1, "dve"),
            ("quant_w_time", 0),
            ("quant_h", 0, 1),
            ("quant_w_time", 1),
            ("step_gain", 1, 1, 0),
            ("turn_x", 4),
            ("turn_x", 5),
            ("empty_x", 4, "act"),
            ("empty_x", 5, "act"),
        ]
    )
    for s in range(2, STEPS):
        first = True
        y_tile = (s - 3) // 2
        turns = []
        if y_tile >= 0:
            turns.append(("y", y_tile, 2 * ((s - 3) % 2)))
            turns.append(("y", y_tile, 2 * ((s - 3) % 2) + 1))
        if s == 2:
            turns.extend(("x", n) for n in range(6, s + X_LEAD))
        if s + X_LEAD < STEPS:
            turns.append(("x", s + X_LEAD))
        on_dve = turns[: DVE_TURNS[s % len(DVE_TURNS)]]
        on_act = turns[len(on_dve) :]
        if first:
            add(("layer1", s, 0, 0))
            add(("layer1", s, 0, 1))
            add(("layer1", s, 1, 0))
            add(("layer1", s, 1, 1))
        if s == 2:
            add(("layer2", 0, 0))
            add(("layer2", 0, 1))
            add(("quant_x", 2, None))
        for turn in turns:
            add(("turn_" + turn[0],) + turn[1:])
        add(("quant_h", s - 1, 1))
        add(("quant_h", s - 1, 0))
        if on_dve:
            add(("empty_" + on_dve[0][0],) + on_dve[0][1:] + ("dve",))
        if first:
            add(("step_gain", s, 0, POOL_COLS))
        for turn in on_dve[1:]:
            add(("empty_" + turn[0],) + turn[1:] + ("dve",))
        if first:
            add(("step_gain", s, 1, 0))
        for turn in on_act:
            add(("empty_" + turn[0],) + turn[1:] + ("act",))
        if s == 2:
            add(("gain", 0, 0))
            add(("gain", 0, 1))
        if s == STEPS - 1:
            break
        if y_tile >= 0 and s % 2 == 1:
            add(("group_y", y_tile, 0))
            add(("group_y", y_tile, 1))
        if y_tile >= 0 and s % 2 == 0:
            add(("quant_y", y_tile, None))
        if s == 3:
            add(("quant_x", 3, None))
        if s % 2 == 0 and s >= 4 and s + 4 < STEPS:
            add(("quant_x", (s + 4) // 2, None))
        add(("layer2", s - 1, 0))
        add(("layer2", s - 1, 1))
        add(("gain", s - 1, 0))
        add(("gain", s - 1, 1))
    order.extend(
        [
            ("layer2", 14, 0),
            ("layer2", 14, 1),
            ("quant_h", 15, 0),
            ("quant_h", 15, 1),
            ("turn_y", 6, 2),
            ("turn_y", 6, 3),
            ("layer2", 15, 0),
            ("layer2", 15, 1),
            ("gain", 14, 0),
            ("gain", 14, 1),
            ("group_y", 6, 0),
            ("group_y", 6, 1),
            ("gain", 15, 0),
            ("gain", 15, 1),
            ("turn_y", 7, 0),
            ("turn_y", 7, 1),
            ("turn_y", 7, 2),
            ("turn_y", 7, 3),
            ("quant_y", 6, None),
            ("group_y", 7, 0),
            ("group_y", 7, 1),
            ("empty_y", 7, 0, "act"),
            ("empty_y", 7, 1, "act"),
            ("empty_y", 7, 2, "act"),
            ("empty_y", 7, 3, "act"),
            ("quant_y", 7, None),
        ]
    )
    order.insert(order.index(("layer2", 15, 0)), ("empty_y", 6, 2, "act"))
    order.insert(order.index(("layer2", 15, 0)), ("empty_y", 6, 3, "act"))
    return order


def tile_observation_history_policy_trunk_h3_kernel(
    tc, obs, w_in, step_gain, w_time, bias, gain, out_0, out_1, out_2
):
    nc = tc.nc
    with ExitStack() as ctx:
        keep = ctx.enter_context(tc.tile_pool(name="keep", bufs=1))
        work = ctx.enter_context(tc.tile_pool(name="work", bufs=3))
        psum = ctx.enter_context(tc.psum_pool(name="psum", bufs=1))
        ctx.enter_context(tc.manual_schedule())

        ident = keep.tile([P, P], F32, name="ident")
        make_identity(nc, ident[:])

        vec_rows = keep.tile([P, K_PASS], BF16, name="vec_rows")
        nc.vector.memset(vec_rows[:].bitcast(I32), 0)
        vec_bank = psum.tile([P, 2, P], F32, name="vec_bank")
        vec_turned = vec_bank[:].bitcast(BF16).rearrange("p u (r e) -> p r u e", e=2)
        vec = keep.tile([P, 6, 2, 2], F32, name="vec")
        warm = keep.tile([P, 1], F32, name="warm")
        zero = keep.tile([P, 1], F32, name="zero")
        nc.vector.memset(zero[:], 0.0)
        nc.scalar.activation(out=warm[:], in_=zero[:], func=TANH)

        w_in_codes = keep.tile([P, F], U32, name="w_in_codes", align_bytes=64)
        w_in_scales = keep.tile([P, F], U8, name="w_in_scales", align_bytes=64)
        w_time_codes = keep.tile([P, 2, S], U32, name="w_time_codes", align_bytes=64)
        w_time_scales = keep.tile([P, 2, S], U8, name="w_time_scales", align_bytes=64)

        tiles = {}
        copy_on = {"act": nc.scalar.copy, "dve": nc.vector.tensor_copy}
        banks_used = []

        def new_bank():
            n = len(banks_used)
            banks_used.append(n)
            return psum.tile([P, BANK], F32, name="bank%d" % (n % BANKS))

        def load_x(half, pair):
            if pair != 1:
                tiles["x_raw", half] = keep.tile([P, PACK * D], BF16, name="x_raw%d" % half)
            cols = slice(0, PACK * D) if pair is None else slice(pair * 2 * D, (pair + 1) * 2 * D)
            rows = obs[half // 2, (half % 2) * K_PASS : (half % 2 + 1) * K_PASS, :]
            nc.sync.dma_start(
                out=tiles["x_raw", half][:, cols],
                in_=rows.rearrange("(m t) c -> m (t c)", t=PACK)[:, cols],
            )

        def load_vectors():
            for k, v in enumerate((step_gain, bias, gain)):
                nc.sync.dma_start(out=vec_rows[2 * k : 2 * k + 2, :], in_=v.rearrange("(g c) -> g c", g=2))

        def load_w_in(g):
            raw = keep.tile([P, PACK, K_PASS], BF16, name="w_in_raw%d" % g)
            cols = w_in[:, g * K_PASS : (g + 1) * K_PASS]
            nc.sync.dma_start(out=raw[:], in_=cols.rearrange("(p j) f -> p j f", j=PACK))
            tiles["w_in_raw", g] = raw

        def load_w_time(half):
            raw = keep.tile([P, PACK, S], BF16, name="w_time_raw%d" % half)
            rows = w_time[half * K_PASS : (half + 1) * K_PASS, :]
            nc.sync.dma_start(out=raw[:], in_=rows.rearrange("(p j) s -> p j s", j=PACK))
            tiles["w_time_raw", half] = raw

        def vectors():
            words = vec_rows[:].bitcast(F32)
            for u in range(2):
                nc.tensor.transpose(vec_bank[:, u, :], words[:, u : 2 * P : 2], ident[:])
            nc.vector.tensor_copy(out=vec[:], in_=vec_turned[:, 0:6, :, :])

        def group_w_in(chunk, engine):
            grouped = work.tile([P, CHUNK * PACK], BF16, name="w_in_grouped", bufs=2, align_bytes=64)
            raw = tiles["w_in_raw", chunk // 2][:].rearrange("p j (m t) -> p t m j", t=PACK)
            t0 = 2 * (chunk % 2)
            copy_on[engine](
                out=grouped[:].rearrange("p (t m j) -> p t m j", t=2, j=PACK),
                in_=raw[:, t0 : t0 + 2, :, :],
            )
            tiles["w_in_grouped", chunk] = grouped

        def quant_w_in(chunk):
            cols = slice(chunk * CHUNK, (chunk + 1) * CHUNK)
            nc.vector.quantize_mx(
                out=w_in_codes[:, cols].bitcast(FP8X4),
                scales=w_in_scales[:, cols],
                in_=tiles["w_in_grouped", chunk][:],
            )

        def group_w_time(half, engine):
            grouped = work.tile([P, S * PACK], BF16, name="w_time_grouped", bufs=2, align_bytes=64)
            copy_on[engine](
                out=grouped[:].rearrange("p (c i j) -> p c j i", i=4, j=PACK),
                in_=tiles["w_time_raw", half][:].rearrange("p j (c i) -> p c j i", i=4),
            )
            tiles["w_time_grouped", half] = grouped

        def quant_w_time(half):
            nc.vector.quantize_mx(
                out=w_time_codes[:, half, :].bitcast(FP8X4),
                scales=w_time_scales[:, half, :],
                in_=tiles["w_time_grouped", half][:],
            )

        def turn_x(n):
            half, pair = divmod(n, 2)
            if pair == 0:
                tiles["x_grouped", half] = work.tile(
                    [P, PACK * K_PASS], BF16, name="x_grouped", bufs=2, align_bytes=64
                )
            words = tiles["x_raw", half][:].bitcast(F32)
            bank = new_bank()
            for e in range(2):
                t = 2 * pair + e
                for u in range(2):
                    slot = 2 * e + u
                    nc.tensor.transpose(
                        bank[:, slot * P : (slot + 1) * P],
                        words[:, 256 * t + u : 256 * (t + 1) : 2],
                        ident[:],
                    )
            tiles["x_bank", n] = bank

        def empty_x(n, engine):
            half, pair = divmod(n, 2)
            bank = tiles["x_bank", n]
            grouped = tiles["x_grouped", half][:].bitcast(F32)
            copy_on[engine](
                out=grouped[:, pair * BANK : (pair + 1) * BANK].rearrange("p (e m u) -> p e m u", e=2, u=2),
                in_=bank[:].rearrange("p (e u m) -> p e m u", e=2, u=2),
            )

        def quant_x(half, pair):
            if pair != 1:
                codes = work.tile([P, K_PASS], U32, name="x_codes", bufs=4, align_bytes=64)
                scales = work.tile([P, K_PASS], U8, name="x_scales", bufs=4, align_bytes=64)
                tiles["x_mx", half] = (codes, scales)
            codes, scales = tiles["x_mx", half]
            lo, hi = (0, K_PASS) if pair is None else (pair * 2 * P, (pair + 1) * 2 * P)
            nc.vector.quantize_mx(
                out=codes[:, lo:hi].bitcast(FP8X4),
                scales=scales[:, lo:hi],
                in_=tiles["x_grouped", half][:, PACK * lo : PACK * hi],
            )

        def layer1(s, h, u):
            b, chunk = divmod(s, 4)
            codes, scales = tiles["x_mx", 2 * b + h]
            cols = slice(chunk * CHUNK, (chunk + 1) * CHUNK)
            bank = new_bank()
            for e in range(2):
                ticks = slice((2 * u + e) * P, (2 * u + e + 1) * P)
                nc.tensor.matmul_mx(
                    out=bank[:, e * CHUNK : (e + 1) * CHUNK],
                    lhsT=codes[:, ticks].bitcast(FP8X4),
                    lhsT_scale=scales[:, ticks],
                    rhs=w_in_codes[:, cols].bitcast(FP8X4),
                    rhs_scale=w_in_scales[:, cols],
                    start=True,
                    stop=True,
                )
            if u == 0:
                tiles["tanh_a", s, h] = work.tile([P, 2, CHUNK, 2], F32, name="tanh_a", bufs=4)
            nc.scalar.activation(
                out=tiles["tanh_a", s, h][:, u, :, :],
                in_=bank[:].rearrange("p (e n) -> p n e", e=2),
                func=TANH,
            )

        def step_gain_mul(s, h, split):
            h_tile = work.tile([P, CHUNK, 2, 2], BF16, name="h%d" % h, bufs=1, align_bytes=64)
            tiles["h", s, h] = h_tile
            tanh_a = tiles["tanh_a", s, h][:].rearrange("p u n e -> p n u e")
            if split > 0:
                nc.gpsimd.tensor_tensor(
                    out=h_tile[:, 0:split, :, :],
                    in0=tanh_a[:, 0:split, :, :],
                    in1=vec[:, h : h + 1, :, :].to_broadcast([P, split, 2, 2]),
                    op=MULT,
                )
            if split < CHUNK:
                nc.vector.tensor_tensor(
                    out=h_tile[:, split:CHUNK, :, :],
                    in0=tanh_a[:, split:CHUNK, :, :],
                    in1=vec_turned[:, h : h + 1, :, :].to_broadcast([P, CHUNK - split, 2, 2]),
                    op=MULT,
                )

        def quant_h(s, h):
            if ("h_mx", s) not in tiles:
                codes = work.tile([P, 2 * CHUNK], U32, name="h_codes", bufs=3, align_bytes=64)
                scales = work.tile([P, 2 * CHUNK], U8, name="h_scales", bufs=3, align_bytes=64)
                tiles["h_mx", s] = (codes, scales)
            codes, scales = tiles["h_mx", s]
            cols = slice(h * CHUNK, (h + 1) * CHUNK)
            nc.vector.quantize_mx(
                out=codes[:, cols].bitcast(FP8X4),
                scales=scales[:, cols],
                in_=tiles["h", s, h][:].rearrange("p n u e -> p (n u e)"),
            )

        def layer2(s, e):
            codes, scales = tiles["h_mx", s]
            bank = new_bank()
            for h in range(2):
                feats = slice(h * CHUNK + e * P, h * CHUNK + (e + 1) * P)
                nc.tensor.matmul_mx(
                    out=bank[:],
                    lhsT=codes[:, feats].bitcast(FP8X4),
                    lhsT_scale=scales[:, feats],
                    rhs=w_time_codes[:, h, :].bitcast(FP8X4),
                    rhs_scale=w_time_scales[:, h, :],
                    start=(h == 0),
                    stop=(h == 1),
                )
            g, u = divmod(s % 4, 2)
            tanh_z = work.tile([P, S], F32, name="tanh_z", bufs=4)
            nc.scalar.activation(out=tanh_z[:], in_=bank[:], func=TANH, bias=vec[:, 2 + g, u, e : e + 1])
            tiles["tanh_z", s, e] = tanh_z

        def gain_mul(s, e):
            if s % 2 == 0 and e == 0:
                tiles["y", s // 2] = work.tile([P, PACK, S], F32, name="y", bufs=3)
            g, u = divmod(s % 4, 2)
            nc.vector.tensor_scalar(
                out=tiles["y", s // 2][:, 2 * u + e, :],
                in0=tiles["tanh_z", s, e][:],
                scalar1=vec[:, 4 + g, u, e : e + 1],
                scalar2=None,
                op0=MULT,
            )

        def group_y(n, part):
            if part == 0:
                tiles["y_grouped", n] = work.tile(
                    [P, S * PACK], BF16, name="y_grouped", bufs=2, align_bytes=64
                )
            half = S // 2
            nc.vector.tensor_copy(
                out=tiles["y_grouped", n][:, part * half * PACK : (part + 1) * half * PACK].rearrange(
                    "p (c i t) -> p c t i", i=4, t=PACK
                ),
                in_=tiles["y", n][:, :, part * half : (part + 1) * half].rearrange(
                    "p t (c i) -> p c t i", i=4
                ),
            )

        def quant_y(n, part):
            b, g = divmod(n, 2)
            if part != 1:
                tiles["y_codes", n] = work.tile([P, S], U32, name="y_codes", bufs=2, align_bytes=64)
            if ("y_scales", b) not in tiles:
                tiles["y_scales", b] = work.tile([P, 2, S], U8, name="y_scales", bufs=2, align_bytes=64)
            codes, scales = tiles["y_codes", n], tiles["y_scales", b]
            lo, hi = (0, S) if part is None else (part * S // 2, (part + 1) * S // 2)
            nc.vector.quantize_mx(
                out=codes[:, lo:hi].bitcast(FP8X4),
                scales=scales[:, g, lo:hi],
                in_=tiles["y_grouped", n][:, PACK * lo : PACK * hi],
            )
            nc.sync.dma_start(
                out=out_1[g, :, b * S + lo : b * S + hi, :].rearrange("p m t -> p (m t)").bitcast(I32),
                in_=codes[:, lo:hi].bitcast(I32),
            )
            if g == 1 and part != 0:
                for q in range(4):
                    rows = out_2[:, 4 * q : 4 * q + 4, b * S : (b + 1) * S]
                    nc.sync.dma_start(
                        out=rows.rearrange("g r m -> r g m").bitcast(I32),
                        in_=scales[32 * q : 32 * q + 4, :, :].bitcast(I32),
                    )

        def turn_y(n, c):
            bank = new_bank()
            for t in range(PACK):
                nc.tensor.transpose(
                    bank[:, t * P : (t + 1) * P], tiles["y", n][:, t, c * P : (c + 1) * P], ident[:]
                )
            tiles["y_bank", n, c] = bank

        def empty_y(n, c, engine):
            b, g = divmod(n, 2)
            bank = tiles["y_bank", n, c]
            if c % 2 == 0:
                tiles["y_rows", n, c // 2] = work.tile([P, 2, K_PASS], F32, name="y_rows", bufs=4)
            rows = tiles["y_rows", n, c // 2]
            copy_on[engine](
                out=rows[:, c % 2, :].rearrange("j (p t) -> j p t", t=PACK),
                in_=bank[:].rearrange("j (t p) -> j p t", t=PACK),
            )
            if c % 2 == 1:
                dst = out_0[b, (c - 1) * P : (c + 1) * P, g * K_PASS : (g + 1) * K_PASS]
                nc.sync.dma_start(out=dst.rearrange("(c j) f -> j c f", c=2), in_=rows[:])

        emit = {
            "load_x": load_x,
            "load_vectors": load_vectors,
            "load_w_in": load_w_in,
            "load_w_time": load_w_time,
            "vectors": vectors,
            "group_w_in": group_w_in,
            "quant_w_in": quant_w_in,
            "group_w_time": group_w_time,
            "quant_w_time": quant_w_time,
            "turn_x": turn_x,
            "quant_x": quant_x,
            "layer1": layer1,
            "step_gain": step_gain_mul,
            "quant_h": quant_h,
            "layer2": layer2,
            "gain": gain_mul,
            "group_y": group_y,
            "quant_y": quant_y,
            "turn_y": turn_y,
            "empty_x": empty_x,
            "empty_y": empty_y,
        }
        for step in program_order():
            emit[step[0]](*step[1:])
